import numpy as np
import ml_dtypes


def mxq(x, axis, fmt="e4m3"):
    dtype, down = {"e4m3": (ml_dtypes.float8_e4m3fn, 7), "e5m2": (ml_dtypes.float8_e5m2, 14)}[fmt]
    v = np.moveaxis(np.asarray(x, np.float32).astype(ml_dtypes.bfloat16).astype(np.float64), axis, -1)
    blocks = v.reshape(v.shape[:-1] + (-1, 32))
    amax = np.abs(blocks).max(-1, keepdims=True)
    byte = np.maximum(np.where(amax > 0, np.frexp(amax)[1] - 1 + 127, 0) - down, 1)
    scale = np.exp2(byte - 127.0)
    codes = (blocks / scale).astype(np.float32).astype(dtype).astype(np.float64)
    return np.moveaxis((codes * scale).reshape(v.shape), -1, axis)


WIDE = False


def mx_kscale(k):
    if not WIDE:
        return np.ones(k)
    levels = np.array([10, -10, 5, -5, 0])
    if k % 512:
        return np.exp2(np.random.permutation(np.resize(levels, k // 32))).repeat(32)
    a = np.empty((k // 512, 16))
    for p in range(k // 512):
        a[p, :8] = np.random.permutation(np.resize(levels, 8))
        for g in range(8):
            far = levels[np.abs(levels - a[p, g]) >= 10]
            a[p, g + 8] = far[np.random.randint(len(far))]
    return np.exp2(a.ravel()).repeat(32)


BF16 = ml_dtypes.bfloat16


def bf(x):
    return np.asarray(x, np.float32).astype(BF16)


def f64(x):
    return np.asarray(x).astype(np.float64)


E2M1 = np.array([0.0, 0.5, 1.0, 1.5, 2.0, 3.0, 4.0, 6.0, -0.0, -0.5, -1.0, -1.5, -2.0, -3.0, -4.0, -6.0])


def pack_weight(w, fmt):
    k, n = w.shape
    w = f64(bf(w)).reshape(k // 32, 32, n)
    amax = np.abs(w).max(1)
    if fmt == "e4m3":
        byte = np.frexp(amax)[1] - 1 + 127 - 7
    else:
        mant, ex = np.frexp(amax / 6.0)
        byte = np.where(mant > 0.5, ex, ex - 1) + 127
    byte = np.clip(np.where(amax > 0, byte, 1), 1, 254)
    scaled = (w * np.exp2(127.0 - byte)[:, None, :]).reshape(k, n).astype(np.float32)
    by_word = np.ascontiguousarray(scaled.reshape(k // 512, 128, 4, n).transpose(0, 1, 3, 2))
    if fmt == "e4m3":
        words = by_word.astype(ml_dtypes.float8_e4m3fn).view(np.uint8)
    else:
        c = by_word.astype(ml_dtypes.float4_e2m1fn).view(np.uint8) & 0xF
        words = c[..., 0::2] | (c[..., 1::2] << 4)
    return np.ascontiguousarray(words), np.ascontiguousarray(byte.astype(np.uint8).reshape(k // 512, 16, n))


def unpack_weight(words, scales, fmt):
    g, p, n, _ = words.shape
    if fmt == "e4m3":
        vals = np.ascontiguousarray(words).view(ml_dtypes.float8_e4m3fn).astype(np.float64)
    else:
        nib = np.empty((g, p, n, 4), np.uint8)
        nib[..., 0::2] = words & 0xF
        nib[..., 1::2] = words >> 4
        vals = E2M1[nib]
    vals = vals * np.repeat(np.exp2(scales.astype(np.float64) - 127.0), 8, axis=1)[..., None]
    return vals.transpose(0, 1, 3, 2).reshape(g * 512, n)
def pack4(w):
    words, scales = pack_weight(w, "e2m1")
    return words.reshape(words.shape[0], 128, -1), scales


def unpack4(words, scales):
    return unpack_weight(words.reshape(words.shape[0], 128, -1, 2), scales, "e2m1")


L, T, D, V = 4, 256, 1024, 2048


def setup_inputs():
    s = mx_kscale(L * D)
    t = mx_kscale(D)
    h = np.random.standard_normal((L * D, T)) * s[:, None]
    a = np.random.standard_normal((L * D, D)) / np.sqrt(D) / s[:, None] * t
    u = np.random.standard_normal((D, V)) / np.sqrt(D) / t[:, None]
    h_words, h_scales = pack4(h)
    a_words, a_scales = pack4(a)
    u_words, u_scales = pack_weight(u, "e4m3")
    return {"h_words": h_words, "h_scales": h_scales,
            "a_words": a_words, "a_scales": a_scales,
            "b": bf(0.4 * np.random.standard_normal((L, D)) * t),
            "r": bf(np.exp(0.3 * np.random.standard_normal((L, T)))),
            "u_words": u_words, "u_scales": u_scales}


def reference(h_words, h_scales, a_words, a_scales, b, r, u_words, u_scales):
    h = unpack4(h_words, h_scales).reshape(L, D, T)
    a = unpack4(a_words, a_scales).reshape(L, D, D)
    u = unpack_weight(u_words, u_scales, "e4m3")
    y = h.swapaxes(1, 2) @ a
    z = (y + f64(b)[:, None, :]) * f64(r)[:, :, None]
    logits = mxq(z.reshape(L * T, D), 1, "e4m3") @ u
    return logits.reshape(L, T, V)

from contextlib import ExitStack

import concourse.mybir as mybir
from concourse.masks import make_identity

F32 = mybir.dt.float32
BF16 = mybir.dt.bfloat16
I32 = mybir.dt.int32
U32 = mybir.dt.uint32
U8 = mybir.dt.uint8
E4M3 = mybir.dt.float8_e4m3fn_x4
E2M1 = mybir.dt.float4_e2m1fn_x4
MULT = mybir.AluOpType.mult
ADD = mybir.AluOpType.add
COPY = mybir.ActivationFunctionType.Copy

L, T, D, V = 4, 256, 1024, 2048
FLOPS = 2 * L * T * D * D + 2 * L * T * D * V
P = 128


def tile_tuned_logit_lens_s4_kernel(
    tc, h_words, h_scales, a_words, a_scales, b, r, u_words, u_scales, out
):
    nc = tc.nc
    with ExitStack() as ctx:
        keep = ctx.enter_context(tc.tile_pool(name="keep", bufs=1))
        zpool = ctx.enter_context(tc.tile_pool(name="zpool", bufs=4))
        opool = ctx.enter_context(tc.tile_pool(name="opool", bufs=6))
        psum = ctx.enter_context(tc.psum_pool(name="psum", bufs=1))
        ctx.enter_context(tc.manual_schedule())

        def bank(tag, bufs):
            t = psum.tile([P, 512], F32, name=tag, tag=tag, bufs=bufs)
            return t

        ident = keep.tile([P, P], F32, name="ident")
        prm = keep.tile([P, 384], F32, name="prm")
        r_in = keep.tile([8, 128], BF16, name="r_in")
        prm_c = keep.tile([P, 3, 8], F32, name="prm_c")
        warm = keep.tile([P, 1], F32, name="warm")
        hs = keep.tile([P, 8, 256], U8, name="hs", align_bytes=64)
        as0 = keep.tile([P, 2, 1024], U8, name="as0", align_bytes=64)
        as1 = keep.tile([P, 6, 1024], U8, name="as1", align_bytes=64)
        us = keep.tile([P, 2048], U8, name="us", align_bytes=64)
        hw = [keep.tile([P, 2, 512], U8, name=f"hw{l}", align_bytes=64) for l in range(L)]
        aw = [keep.tile([P, 2, 2048], U8, name=f"aw{l}", align_bytes=64) for l in range(L)]
        uw = [
            [keep.tile([P, 1024], U32, name=f"uw{g}{vh}", align_bytes=64) for vh in range(2)]
            for g in range(2)
        ]
        br = [keep.tile([P, 1024], F32, name=f"br{c}") for c in range(8)]
        bb = {l: keep.tile([P, 1024], BF16, name=f"bb{l}") for l in (2, 3)}

        nc.vector.memset(prm[:], 0.0)
        nc.vector.memset(hs[:].rearrange("p g n -> p (g n)").bitcast(I32), 0)
        nc.vector.memset(as0[:].rearrange("p g n -> p (g n)").bitcast(I32), 0)
        nc.vector.memset(as1[:].rearrange("p g n -> p (g n)").bitcast(I32), 0)
        nc.vector.memset(us[:].bitcast(I32), 0)

        nc.scalar.dma_start(out=r_in[:], in_=r.rearrange("l (t n) -> (l t) n", n=P))
        nc.scalar.dma_start(
            out=prm[0:8, 0:256].bitcast(BF16), in_=b.rearrange("l (g c) -> (l g) c", g=2)
        )

        def scale_rows(queue, plane, src, k):
            queue.dma_start(
                out=plane[k:P:32, :, :].bitcast(I32),
                in_=src.rearrange("g (q k) n -> k q g n", k=4)[k].bitcast(I32),
            )

        def load_h(l):
            nc.sync.dma_start(
                out=hw[l][:].bitcast(I32),
                in_=h_words[2 * l : 2 * l + 2].rearrange("g p n -> p g n").bitcast(I32),
            )

        def load_a(l):
            nc.sync.dma_start(
                out=aw[l][:].bitcast(I32),
                in_=a_words[2 * l : 2 * l + 2].rearrange("g p n -> p g n").bitcast(I32),
            )

        for k in range(4):
            scale_rows(nc.scalar, hs, h_scales, k)
        load_h(0)
        load_a(0)
        for k in range(4):
            scale_rows(nc.gpsimd if k < 2 else nc.scalar, as0, a_scales[0:2], k)
        make_identity(nc, ident[:])
        load_h(1)
        load_a(1)
        for k in range(4):
            scale_rows(nc.sync, as1, a_scales[2:8], k)
        for vh in range(2):
            for g in range(2):
                nc.sync.dma_start(
                    out=uw[g][vh][:].bitcast(I32),
                    in_=u_words[g, :, vh * 1024 : (vh + 1) * 1024, :]
                    .rearrange("p n t -> p (n t)")
                    .bitcast(I32),
                )
        for q in range(4):
            nc.gpsimd.dma_start(
                out=us[32 * q : 32 * q + 8, :].bitcast(I32),
                in_=u_scales[:, 4 * q : 4 * q + 4, :].bitcast(I32),
            )
        for l in (2, 3):
            load_h(l)
            load_a(l)

        nc.vector.memset(warm[:], 0.0)
        nc.scalar.activation(out=warm[:], in_=warm[:], func=COPY)
        nc.vector.tensor_copy(out=prm[0:8, 256:384], in_=r_in[:])
        tp = bank("t", 2)
        nc.tensor.transpose(tp[:, 0:128], prm[:, 0:256:2], ident[:])
        nc.tensor.transpose(tp[:, 128:256], prm[:, 1:256:2], ident[:])
        nc.tensor.transpose(tp[:, 256:384], prm[:, 256:384], ident[:])
        nc.vector.tensor_copy(
            out=prm_c[:], in_=tp[:, 0:384].rearrange("p (k n) -> p k n", k=3)[:, :, 0:8]
        )

        def r_col(c):
            return prm_c[:, 2, c : c + 1]

        def spread_b(l, tag, bufs):
            bk = bank(tag, bufs)
            for g in range(2):
                for u in range(2):
                    o = (2 * g + u) * P
                    nc.tensor.transpose(
                        bk[:, o : o + P],
                        prm_c[:, u, 2 * l + g : 2 * l + g + 1].to_broadcast([P, P]),
                        ident[:],
                    )
            return bk

        def keep_b(l, bk):
            nc.scalar.copy(bb[l][:].bitcast(F32), bk[:])

        def make_br(c):
            nc.vector.tensor_scalar(
                out=br[c][:], in0=bb[c // 2][:], scalar1=r_col(c), scalar2=None, op0=MULT
            )

        z = {}
        zc = {}
        zs = {}
        zt = {}
        zi = {}
        ot = {}

        def stage1(c, g):
            l, i = divmod(c, 2)
            y = bank("y", 3)
            for k in range(2):
                if l == 0:
                    a_sc = as0[:, k, 512 * g : 512 * (g + 1)]
                else:
                    a_sc = as1[:, 2 * l - 2 + k, 512 * g : 512 * (g + 1)]
                nc.tensor.matmul_mx(
                    out=y[:],
                    lhsT=hw[l][:, k, 256 * i : 256 * (i + 1)].bitcast(E2M1),
                    lhsT_scale=hs[:, 2 * l + k, P * i : P * (i + 1)],
                    rhs=aw[l][:, k, 1024 * g : 1024 * (g + 1)].bitcast(E2M1),
                    rhs_scale=a_sc,
                    start=(k == 0),
                    stop=(k == 1),
                )
            if g == 0:
                zz = zpool.tile([P, 1024], BF16, name="z", tag="z")
                z[c] = zz
            for u in range(2):
                cols = slice(512 * g + 256 * u, 512 * g + 256 * (u + 1))
                nc.vector.scalar_tensor_tensor(
                    out=z[c][:, cols].rearrange("q (p e) -> q p e", e=2),
                    in0=y[:].rearrange("q (p u e) -> q u p e", u=2, e=2)[:, u],
                    scalar=r_col(c),
                    in1=br[c][:, cols].rearrange("q (p e) -> q p e", e=2),
                    op0=MULT,
                    op1=ADD,
                )

        def turn(c):
            t = bank("t", 2)
            words = z[c][:].bitcast(F32)
            for k in range(4):
                nc.tensor.transpose(t[:, P * k : P * (k + 1)], words[:, P * k : P * (k + 1)], ident[:])
            zt[c] = t

        def lay(c):
            t = zpool.tile([P, 1024], BF16, name="zi", tag="zi", align_bytes=64)
            nc.scalar.copy(
                t[:].bitcast(F32).rearrange("q (g n u) -> q g n u", g=2, u=2),
                zt[c][:].rearrange("q (g u n) -> q g n u", g=2, u=2),
            )
            zi[c] = t

        def quant(c):
            codes = zpool.tile([P, 256], U32, name="zc", tag="zc", align_bytes=64)
            scales = zpool.tile([P, 256], U8, name="zs", tag="zs", align_bytes=64)
            nc.vector.quantize_mx(out=codes[:].bitcast(E4M3), scales=scales[:], in_=zi[c][:])
            zc[c] = codes
            zs[c] = scales

        def stage2(c, v, on_vector):
            l, i = divmod(c, 2)
            acc = bank("s", 3)
            for g in range(2):
                nc.tensor.matmul_mx(
                    out=acc[:],
                    lhsT=zc[c][:, P * g : P * (g + 1)].bitcast(E4M3),
                    lhsT_scale=zs[c][:, P * g : P * (g + 1)],
                    rhs=uw[g][v // 2][:, 512 * (v % 2) : 512 * (v % 2 + 1)].bitcast(E4M3),
                    rhs_scale=us[4 * g : P, 512 * v : 512 * (v + 1)],
                    start=(g == 0),
                    stop=(g == 1),
                )
            if v == 0:
                o = opool.tile([P, 2048], F32, name="o", tag="o")
                ot[c] = o
            dst = ot[c][:, 512 * v : 512 * (v + 1)]
            if on_vector:
                nc.vector.tensor_copy(out=dst, in_=acc[:])
            else:
                nc.scalar.copy(dst, acc[:])
            if v % 2 == 1:
                cols = slice(512 * (v - 1), 512 * (v + 1))
                nc.sync.dma_start(out=out[l, P * i : P * (i + 1), cols], in_=ot[c][:, cols])

        bk = spread_b(0, "t", 2)
        nc.scalar.activation(out=br[0][:], in_=bk[:].bitcast(BF16), func=COPY, scale=r_col(0))
        nc.vector.tensor_scalar(
            out=br[1][:], in0=bk[:].bitcast(BF16), scalar1=r_col(1), scalar2=None, op0=MULT
        )
        bk = spread_b(1, "s", 3)
        for c in (2, 3):
            nc.scalar.activation(out=br[c][:], in_=bk[:].bitcast(BF16), func=COPY, scale=r_col(c))
        for c in (0, 1):
            for g in range(2):
                stage1(c, g)
        stage1(2, 0)
        stage1(2, 1)
        turn(0)
        turn(1)
        lay(0)
        lay(1)
        bk2 = spread_b(2, "s", 3)
        bk3 = spread_b(3, "s", 3)
        quant(0)
        stage1(3, 0)
        quant(1)
        stage1(3, 1)
        keep_b(2, bk2)
        keep_b(3, bk3)
        for v in range(4):
            stage2(0, v, v == 1)
            stage2(1, v, v == 3)
            if v == 1:
                make_br(4)
                make_br(5)
            if v == 2:
                make_br(6)
                make_br(7)
        turn(2)
        turn(3)
        lay(2)
        lay(3)
        stage1(4, 0)
        quant(2)
        stage1(4, 1)
        quant(3)
        stage1(5, 0)
        stage1(5, 1)
        for c in (2, 3):
            for v in range(4):
                stage2(c, v, v == 2)
        turn(4)
        turn(5)
        lay(4)
        lay(5)
        stage1(6, 0)
        quant(4)
        stage1(6, 1)
        quant(5)
        stage1(7, 0)
        stage1(7, 1)
        for v in range(4):
            stage2(4, v, v == 3)
        turn(6)
        turn(7)
        lay(6)
        lay(7)
        for v in range(4):
            stage2(5, v, v == 0 or v == 3)
            if v == 1:
                quant(6)
                quant(7)
        for c in (6, 7):
            for v in range(4):
                stage2(c, v, v % 2 == 1)
